import numpy as np, ml_dtypes
CORES = [4,12,20,28,36,44,0,8,16,24,32,40]
N = 12
def setup_inputs(rng):
    return {"x": rng.standard_normal((N, 128, 32), dtype=np.float32).astype(ml_dtypes.bfloat16)}
def reference(x):
    g = np.concatenate(list(x), axis=1)
    return {"y": np.broadcast_to(g, (N,) + g.shape)}

@@ -1,0 +1,75 @@
+from concourse.bass import DstId, RemoteDMATransfer
+
+W = 32
+BLK = 6 * W
+
+SCRATCH = {
+    "xd": ("dram", [128, W], "bfloat16"),
+    "G": ("sbuf", [128, BLK], "bfloat16"),
+    "land": ("sbuf", [128, 2 * BLK], "bfloat16"),
+}
+SEMAPHORES = ["ld", "snt", "in_l", "in_r", "in_x", "arr0", "arr1", "st0", "st1"]
+
+HUB = {(0, 0): 6, (0, 1): 14, (1, 0): 18, (1, 1): 26}
+
+
+def _dst(topo, c):
+    rid, pid, _ = topo.addr(c)
+    return DstId(rid=rid, pnc=pid)
+
+
+def rank_program(g, core, T, topo):
+    rank = T.rank_of(core)
+    if rank is not None:
+        blk, slot = divmod(rank, 6)
+        hub = HUB[(blk, topo.chip(core) & 1)]
+        g.sync.dma_start(T.xd[:], T.x[:]).then_inc(T.sem.ld, 16)
+        g.wait_ge(T.sem.ld, 16)
+        rid, pid, _ = topo.addr(hub)
+        local = topo.chip(hub) == topo.chip(core)
+        g.remote_dma(T.G[:, slot * W:(slot + 1) * W], T.xd[:],
+                     remote_sem=T.sem.in_l if local else T.sem.in_r, local_sem=T.sem.snt,
+                     pid=pid, routing_id=rid, dma_engine_mask=0xFFFF if local else 0x00FF)
+        g.sync.wait_ge(T.sem.arr0, 8)
+        g.sync.dma_start(T.y[:, 0:BLK], T.land[:, 0:BLK]).then_inc(T.sem.st0, 16)
+        g.scalar.wait_ge(T.sem.arr1, 8)
+        g.scalar.dma_start(T.y[:, BLK:2 * BLK], T.land[:, BLK:2 * BLK]).then_inc(T.sem.st1, 16)
+        g.wait_ge(T.sem.snt, 16 if local else 8)
+        g.sync.wait_ge(T.sem.st0, 16)
+        g.scalar.wait_ge(T.sem.st1, 16)
+        return
+
+    for (blk, par), hub in HUB.items():
+        if hub != core:
+            continue
+        peer = HUB[(blk, 1 - par)]
+        mine = [r for r in range(6 * blk, 6 * blk + 6) if (topo.chip(T.cores[r]) & 1) == par]
+        near = [r for r in mine if topo.chip(T.cores[r]) == topo.chip(core)]
+        far = [r for r in mine if topo.chip(T.cores[r]) != topo.chip(core)]
+        prid, ppid, _ = topo.addr(peer)
+
+        def col(r):
+            s = r % 6
+            return T.G[:, s * W:(s + 1) * W]
+
+        g.wait_ge(T.sem.in_l, 16)
+        g.remote_dma(col(near[0]), col(near[0]), remote_sem=T.sem.in_x, local_sem=T.sem.snt,
+                     pid=ppid, routing_id=prid, dma_engine_mask=0x00FF)
+        g.wait_ge(T.sem.in_r, 16)
+        g.remote_dma_fused([
+            RemoteDMATransfer(dst_ids=[_dst(topo, peer)], dma_engine_mask=m, remote_sem=T.sem.in_x,
+                              srcs=[col(r)], dsts=[col(r)])
+            for r, m in zip(far, (0x000F, 0x00F0))], local_sem=T.sem.snt)
+        g.wait_ge(T.sem.in_x, 16)
+        arr = T.sem.arr0 if blk == 0 else T.sem.arr1
+        out = T.land[:, blk * BLK:(blk + 1) * BLK]
+        dests = [c for c in T.cores if (topo.chip(c) & 1) == par]
+        off = [c for c in dests if topo.chip(c) != topo.chip(core)]
+        on = [c for c in dests if topo.chip(c) == topo.chip(core)]
+        g.remote_dma_fused([
+            RemoteDMATransfer(dst_ids=[_dst(topo, c) for c in off], dma_engine_mask=0x00FF, remote_sem=arr,
+                              srcs=[T.G[:]], dsts=[out for _ in off]),
+            RemoteDMATransfer(dst_ids=[_dst(topo, c) for c in on], dma_engine_mask=0xFF00, remote_sem=arr,
+                              srcs=[T.G[:]], dsts=[out for _ in on]),
+        ], local_sem=T.sem.snt)
+        g.wait_ge(T.sem.snt, 8 + 8 + 16)

@@ -10,12 +10,19 @@ SCRATCH = {
 }
 SEMAPHORES = ["ld", "snt", "in_l", "in_r", "in_x", "arr0", "arr1", "st0", "st1"]
 
-HUB = {(0, 0): 6, (0, 1): 14, (1, 0): 18, (1, 1): 26}
+HUB = {(0, 0): 6, (0, 1): 30, (1, 0): 18, (1, 1): 42}
 
 
 def _dst(topo, c):
     rid, pid, _ = topo.addr(c)
     return DstId(rid=rid, pnc=pid)
+
+
+def _serves(topo, blk, par):
+    h = topo.chip(HUB[(blk, par)])
+    o = topo.chip(HUB[(blk, 1 - par)])
+    third = [c for c in range(6) if (c & 1) == par and c != h and c != (o ^ 1)]
+    return h, h ^ 1, third[0]
 
 
 def rank_program(g, core, T, topo):
@@ -30,9 +37,10 @@ def rank_program(g, core, T, topo):
         g.remote_dma(T.G[:, slot * W:(slot + 1) * W], T.xd[:],
                      remote_sem=T.sem.in_l if local else T.sem.in_r, local_sem=T.sem.snt,
                      pid=pid, routing_id=rid, dma_engine_mask=0xFFFF if local else 0x00FF)
-        g.sync.wait_ge(T.sem.arr0, 8)
+        n = [8 if topo.chip(core) in (topo.chip(HUB[(b, 0)]), topo.chip(HUB[(b, 1)])) else 4 for b in (0, 1)]
+        g.sync.wait_ge(T.sem.arr0, n[0])
         g.sync.dma_start(T.y[:, 0:BLK], T.land[:, 0:BLK]).then_inc(T.sem.st0, 16)
-        g.scalar.wait_ge(T.sem.arr1, 8)
+        g.scalar.wait_ge(T.sem.arr1, n[1])
         g.scalar.dma_start(T.y[:, BLK:2 * BLK], T.land[:, BLK:2 * BLK]).then_inc(T.sem.st1, 16)
         g.wait_ge(T.sem.snt, 16 if local else 8)
         g.sync.wait_ge(T.sem.st0, 16)
@@ -63,13 +71,11 @@ def rank_program(g, core, T, topo):
         g.wait_ge(T.sem.in_x, 16)
         arr = T.sem.arr0 if blk == 0 else T.sem.arr1
         out = T.land[:, blk * BLK:(blk + 1) * BLK]
-        dests = [c for c in T.cores if (topo.chip(c) & 1) == par]
-        off = [c for c in dests if topo.chip(c) != topo.chip(core)]
-        on = [c for c in dests if topo.chip(c) == topo.chip(core)]
-        g.remote_dma_fused([
-            RemoteDMATransfer(dst_ids=[_dst(topo, c) for c in off], dma_engine_mask=0x00FF, remote_sem=arr,
-                              srcs=[T.G[:]], dsts=[out for _ in off]),
-            RemoteDMATransfer(dst_ids=[_dst(topo, c) for c in on], dma_engine_mask=0xFF00, remote_sem=arr,
-                              srcs=[T.G[:]], dsts=[out for _ in on]),
-        ], local_sem=T.sem.snt)
+        own, mate, third = _serves(topo, blk, par)
+        trs = []
+        for ch, m in ((mate, 0x000F), (third, 0x00F0), (own, 0xFF00)):
+            cs = [c for c in T.cores if topo.chip(c) == ch]
+            trs.append(RemoteDMATransfer(dst_ids=[_dst(topo, c) for c in cs], dma_engine_mask=m, remote_sem=arr,
+                                         srcs=[T.G[:]], dsts=[out for _ in cs]))
+        g.remote_dma_fused(trs, local_sem=T.sem.snt)
         g.wait_ge(T.sem.snt, 8 + 8 + 16)

@@ -10,7 +10,7 @@ SCRATCH = {
 }
 SEMAPHORES = ["ld", "snt", "in_l", "in_r", "in_x", "arr0", "arr1", "st0", "st1"]
 
-HUB = {(0, 0): 6, (0, 1): 30, (1, 0): 18, (1, 1): 42}
+HUB = {(0, 0): 6, (0, 1): 14, (1, 0): 18, (1, 1): 26}
 
 
 def _dst(topo, c):
@@ -18,31 +18,40 @@ def _dst(topo, c):
     return DstId(rid=rid, pnc=pid)
 
 
-def _serves(topo, blk, par):
-    h = topo.chip(HUB[(blk, par)])
-    o = topo.chip(HUB[(blk, 1 - par)])
-    third = [c for c in range(6) if (c & 1) == par and c != h and c != (o ^ 1)]
-    return h, h ^ 1, third[0]
+def _fwd_chip(topo, blk, par):
+    return topo.chip(HUB[(1 - blk, par)])
 
 
 def rank_program(g, core, T, topo):
     rank = T.rank_of(core)
     if rank is not None:
         blk, slot = divmod(rank, 6)
-        hub = HUB[(blk, topo.chip(core) & 1)]
+        chip = topo.chip(core)
+        par = chip & 1
+        hub = HUB[(blk, par)]
         g.sync.dma_start(T.xd[:], T.x[:]).then_inc(T.sem.ld, 16)
         g.wait_ge(T.sem.ld, 16)
         rid, pid, _ = topo.addr(hub)
-        local = topo.chip(hub) == topo.chip(core)
+        local = topo.chip(hub) == chip
         g.remote_dma(T.G[:, slot * W:(slot + 1) * W], T.xd[:],
                      remote_sem=T.sem.in_l if local else T.sem.in_r, local_sem=T.sem.snt,
                      pid=pid, routing_id=rid, dma_engine_mask=0xFFFF if local else 0x00FF)
-        n = [8 if topo.chip(core) in (topo.chip(HUB[(b, 0)]), topo.chip(HUB[(b, 1)])) else 4 for b in (0, 1)]
+        sent = 16 if local else 8
+        arr = (T.sem.arr0, T.sem.arr1)
+        n = [16 if (b != blk and _fwd_chip(topo, b, par) == chip) else 8 for b in (0, 1)]
+        if _fwd_chip(topo, blk, par) == chip:
+            sib = [c for c in T.cores if topo.chip(c) == chip and c != core][0]
+            srid, spid, _ = topo.addr(sib)
+            g.wait_ge(arr[blk], 8)
+            g.remote_dma(T.land[:, blk * BLK:(blk + 1) * BLK], T.land[:, blk * BLK:(blk + 1) * BLK],
+                         remote_sem=arr[blk], local_sem=T.sem.snt,
+                         pid=spid, routing_id=srid, dma_engine_mask=0xFFFF)
+            sent += 16
         g.sync.wait_ge(T.sem.arr0, n[0])
         g.sync.dma_start(T.y[:, 0:BLK], T.land[:, 0:BLK]).then_inc(T.sem.st0, 16)
         g.scalar.wait_ge(T.sem.arr1, n[1])
         g.scalar.dma_start(T.y[:, BLK:2 * BLK], T.land[:, BLK:2 * BLK]).then_inc(T.sem.st1, 16)
-        g.wait_ge(T.sem.snt, 16 if local else 8)
+        g.wait_ge(T.sem.snt, sent)
         g.sync.wait_ge(T.sem.st0, 16)
         g.scalar.wait_ge(T.sem.st1, 16)
         return
@@ -71,11 +80,17 @@ def rank_program(g, core, T, topo):
         g.wait_ge(T.sem.in_x, 16)
         arr = T.sem.arr0 if blk == 0 else T.sem.arr1
         out = T.land[:, blk * BLK:(blk + 1) * BLK]
-        own, mate, third = _serves(topo, blk, par)
-        trs = []
-        for ch, m in ((mate, 0x000F), (third, 0x00F0), (own, 0xFF00)):
-            cs = [c for c in T.cores if topo.chip(c) == ch]
-            trs.append(RemoteDMATransfer(dst_ids=[_dst(topo, c) for c in cs], dma_engine_mask=m, remote_sem=arr,
-                                         srcs=[T.G[:]], dsts=[out for _ in cs]))
-        g.remote_dma_fused(trs, local_sem=T.sem.snt)
-        g.wait_ge(T.sem.snt, 8 + 8 + 16)
+        fch = _fwd_chip(topo, blk, par)
+        first = [T.cores[r] for r in far if topo.chip(T.cores[r]) == fch][0]
+        off = [c for c in T.cores if (topo.chip(c) & 1) == par and topo.chip(c) not in (fch, topo.chip(core))]
+        on = [c for c in T.cores if topo.chip(c) == topo.chip(core)]
+        frid, fpid, _ = topo.addr(first)
+        g.remote_dma(out, T.G[:], remote_sem=arr, local_sem=T.sem.snt,
+                     pid=fpid, routing_id=frid, dma_engine_mask=0x00FF)
+        g.remote_dma_fused([
+            RemoteDMATransfer(dst_ids=[_dst(topo, c) for c in off], dma_engine_mask=0x00FF, remote_sem=arr,
+                              srcs=[T.G[:]], dsts=[out for _ in off]),
+            RemoteDMATransfer(dst_ids=[_dst(topo, c) for c in on], dma_engine_mask=0xFF00, remote_sem=arr,
+                              srcs=[T.G[:]], dsts=[out for _ in on]),
+        ], local_sem=T.sem.snt)
+        g.wait_ge(T.sem.snt, 8 + 8 + 8 + 16)

@@ -6,11 +6,11 @@ BLK = 6 * W
 SCRATCH = {
     "xd": ("dram", [128, W], "bfloat16"),
     "G": ("sbuf", [128, BLK], "bfloat16"),
-    "land": ("sbuf", [128, 2 * BLK], "bfloat16"),
+    "land": ("dram", [2, 128, BLK], "bfloat16"),
 }
-SEMAPHORES = ["ld", "snt", "in_l", "in_r", "in_x", "arr0", "arr1", "st0", "st1"]
+SEMAPHORES = ["ld", "snt", "inn", "arr0", "arr1", "st0", "st1", "own"]
 
-HUB = {(0, 0): 6, (0, 1): 14, (1, 0): 18, (1, 1): 26}
+SERVE = {6: (0, 1, 4), 18: (2, 3, 5), 46: (5, 4, 1), 26: (3, 2, 0)}
 
 
 def _dst(topo, c):
@@ -18,72 +18,83 @@ def _dst(topo, c):
     return DstId(rid=rid, pnc=pid)
 
 
-def _fwd_chip(topo, blk, par):
-    return topo.chip(HUB[(1 - blk, par)])
+def _hubs(topo, par):
+    return [h for h in SERVE if (topo.chip(h) & 1) == par]
+
+
+def _mask(topo, core, h):
+    hubs = _hubs(topo, topo.chip(core) & 1)
+    if topo.chip(h) == topo.chip(core):
+        return 0xFF00
+    if [o for o in hubs if topo.chip(o) == topo.chip(core)]:
+        return 0x00FF
+    return 0x000F if h == hubs[0] else 0x00F0
+
+
+def _bits(m):
+    return bin(m).count("1")
 
 
 def rank_program(g, core, T, topo):
     rank = T.rank_of(core)
+    chip = topo.chip(core)
     if rank is not None:
-        blk, slot = divmod(rank, 6)
-        chip = topo.chip(core)
         par = chip & 1
-        hub = HUB[(blk, par)]
+        k = rank // 2
         g.sync.dma_start(T.xd[:], T.x[:]).then_inc(T.sem.ld, 16)
+        g.scalar.dma_start(T.y[:, rank * W:(rank + 1) * W], T.x[:]).then_inc(T.sem.own, 16)
         g.wait_ge(T.sem.ld, 16)
-        rid, pid, _ = topo.addr(hub)
-        local = topo.chip(hub) == chip
-        g.remote_dma(T.G[:, slot * W:(slot + 1) * W], T.xd[:],
-                     remote_sem=T.sem.in_l if local else T.sem.in_r, local_sem=T.sem.snt,
-                     pid=pid, routing_id=rid, dma_engine_mask=0xFFFF if local else 0x00FF)
-        sent = 16 if local else 8
+        hubs = _hubs(topo, par)
+        g.remote_dma_fused([
+            RemoteDMATransfer(dst_ids=[_dst(topo, h)], dma_engine_mask=_mask(topo, core, h), remote_sem=T.sem.inn,
+                              srcs=[T.xd[:]], dsts=[T.G[:, k * W:(k + 1) * W]])
+            for h in hubs], local_sem=T.sem.snt)
+        sent = sum(_bits(_mask(topo, core, h)) for h in hubs)
         arr = (T.sem.arr0, T.sem.arr1)
-        n = [16 if (b != blk and _fwd_chip(topo, b, par) == chip) else 8 for b in (0, 1)]
-        if _fwd_chip(topo, blk, par) == chip:
+        st = (T.sem.st0, T.sem.st1)
+        qs = (g.sync, g.scalar)
+        n = [8, 8]
+        fwd = None
+        for q in (0, 1):
+            h = [h for h in _hubs(topo, q) if chip in SERVE[h]][0]
+            if SERVE[h][2] == chip:
+                if topo.die(h) == topo.die(core):
+                    fwd = q
+                else:
+                    n[q] = 16
+        if fwd is not None:
             sib = [c for c in T.cores if topo.chip(c) == chip and c != core][0]
             srid, spid, _ = topo.addr(sib)
-            g.wait_ge(arr[blk], 8)
-            g.remote_dma(T.land[:, blk * BLK:(blk + 1) * BLK], T.land[:, blk * BLK:(blk + 1) * BLK],
-                         remote_sem=arr[blk], local_sem=T.sem.snt,
+            g.wait_ge(arr[fwd], 8)
+            g.remote_dma(T.land[fwd], T.land[fwd], remote_sem=arr[fwd], local_sem=T.sem.snt,
                          pid=spid, routing_id=srid, dma_engine_mask=0xFFFF)
             sent += 16
-        g.sync.wait_ge(T.sem.arr0, n[0])
-        g.sync.dma_start(T.y[:, 0:BLK], T.land[:, 0:BLK]).then_inc(T.sem.st0, 16)
-        g.scalar.wait_ge(T.sem.arr1, n[1])
-        g.scalar.dma_start(T.y[:, BLK:2 * BLK], T.land[:, BLK:2 * BLK]).then_inc(T.sem.st1, 16)
+            qs[fwd].wait_ge(T.sem.snt, sent)
+        cnt = [0, 0]
+        for q in (0, 1):
+            qs[q].wait_ge(arr[q], n[q])
+            for s in range(6):
+                r = 2 * s + q
+                if r == rank:
+                    continue
+                qs[q].dma_start(T.y[:, r * W:(r + 1) * W], T.land[q, :, s * W:(s + 1) * W]).then_inc(st[q], 16)
+                cnt[q] += 16
         g.wait_ge(T.sem.snt, sent)
-        g.sync.wait_ge(T.sem.st0, 16)
-        g.scalar.wait_ge(T.sem.st1, 16)
+        g.sync.wait_ge(T.sem.st0, cnt[0])
+        g.scalar.wait_ge(T.sem.st1, cnt[1])
+        g.scalar.wait_ge(T.sem.own, 16)
         return
 
-    for (blk, par), hub in HUB.items():
-        if hub != core:
-            continue
-        peer = HUB[(blk, 1 - par)]
-        mine = [r for r in range(6 * blk, 6 * blk + 6) if (topo.chip(T.cores[r]) & 1) == par]
-        near = [r for r in mine if topo.chip(T.cores[r]) == topo.chip(core)]
-        far = [r for r in mine if topo.chip(T.cores[r]) != topo.chip(core)]
-        prid, ppid, _ = topo.addr(peer)
-
-        def col(r):
-            s = r % 6
-            return T.G[:, s * W:(s + 1) * W]
-
-        g.wait_ge(T.sem.in_l, 16)
-        g.remote_dma(col(near[0]), col(near[0]), remote_sem=T.sem.in_x, local_sem=T.sem.snt,
-                     pid=ppid, routing_id=prid, dma_engine_mask=0x00FF)
-        g.wait_ge(T.sem.in_r, 16)
-        g.remote_dma_fused([
-            RemoteDMATransfer(dst_ids=[_dst(topo, peer)], dma_engine_mask=m, remote_sem=T.sem.in_x,
-                              srcs=[col(r)], dsts=[col(r)])
-            for r, m in zip(far, (0x000F, 0x00F0))], local_sem=T.sem.snt)
-        g.wait_ge(T.sem.in_x, 16)
-        arr = T.sem.arr0 if blk == 0 else T.sem.arr1
-        out = T.land[:, blk * BLK:(blk + 1) * BLK]
-        fch = _fwd_chip(topo, blk, par)
-        first = [T.cores[r] for r in far if topo.chip(T.cores[r]) == fch][0]
-        off = [c for c in T.cores if (topo.chip(c) & 1) == par and topo.chip(c) not in (fch, topo.chip(core))]
-        on = [c for c in T.cores if topo.chip(c) == topo.chip(core)]
+    if core in SERVE:
+        par = chip & 1
+        own, mate, third = SERVE[core]
+        srcs = [c for c in T.cores if (topo.chip(c) & 1) == par]
+        g.wait_ge(T.sem.inn, sum(_bits(_mask(topo, c, core)) for c in srcs))
+        arr = T.sem.arr0 if par == 0 else T.sem.arr1
+        out = T.land[par]
+        first = [c for c in T.cores if topo.chip(c) == third and topo.die(c) == topo.die(core)][0]
+        off = [c for c in T.cores if topo.chip(c) == mate]
+        on = [c for c in T.cores if topo.chip(c) == own]
         frid, fpid, _ = topo.addr(first)
         g.remote_dma(out, T.G[:], remote_sem=arr, local_sem=T.sem.snt,
                      pid=fpid, routing_id=frid, dma_engine_mask=0x00FF)
@@ -93,4 +104,4 @@ def rank_program(g, core, T, topo):
             RemoteDMATransfer(dst_ids=[_dst(topo, c) for c in on], dma_engine_mask=0xFF00, remote_sem=arr,
                               srcs=[T.G[:]], dsts=[out for _ in on]),
         ], local_sem=T.sem.snt)
-        g.wait_ge(T.sem.snt, 8 + 8 + 8 + 16)
+        g.wait_ge(T.sem.snt, 8 + 8 + 8)

from concourse.bass import DstId, RemoteDMATransfer

W = 32
BLK = 6 * W

SCRATCH = {
    "xd": ("dram", [128, W], "bfloat16"),
    "G": ("sbuf", [128, BLK], "bfloat16"),
    "land": ("dram", [2, 128, BLK], "bfloat16"),
}
SEMAPHORES = ["ld", "snt", "inn", "arr0", "arr1", "st0", "st1", "own"]

SERVE = {6: (0, 1, 4), 18: (2, 3, 5), 46: (5, 4, 1), 26: (3, 2, 0)}


def _dst(topo, c):
    rid, pid, _ = topo.addr(c)
    return DstId(rid=rid, pnc=pid)


def _hubs(topo, par):
    return [h for h in SERVE if (topo.chip(h) & 1) == par]


def _mask(topo, core, h):
    hubs = _hubs(topo, topo.chip(core) & 1)
    if topo.chip(h) == topo.chip(core):
        return 0xFF00
    if [o for o in hubs if topo.chip(o) == topo.chip(core)]:
        return 0x00FF
    return 0x000F if h == hubs[0] else 0x00F0


def _bits(m):
    return bin(m).count("1")


def rank_program(g, core, T, topo):
    rank = T.rank_of(core)
    chip = topo.chip(core)
    if rank is not None:
        par = chip & 1
        k = rank // 2
        g.sync.dma_start(T.xd[:], T.x[:]).then_inc(T.sem.ld, 16)
        g.scalar.dma_start(T.y[:, rank * W:(rank + 1) * W], T.x[:]).then_inc(T.sem.own, 16)
        g.wait_ge(T.sem.ld, 16)
        hubs = _hubs(topo, par)
        g.remote_dma_fused([
            RemoteDMATransfer(dst_ids=[_dst(topo, h)], dma_engine_mask=_mask(topo, core, h), remote_sem=T.sem.inn,
                              srcs=[T.xd[:]], dsts=[T.G[:, k * W:(k + 1) * W]])
            for h in hubs], local_sem=T.sem.snt)
        sent = sum(_bits(_mask(topo, core, h)) for h in hubs)
        arr = (T.sem.arr0, T.sem.arr1)
        st = (T.sem.st0, T.sem.st1)
        qs = (g.sync, g.scalar)
        n = [8, 8]
        fwd = None
        for q in (0, 1):
            h = [h for h in _hubs(topo, q) if chip in SERVE[h]][0]
            if SERVE[h][2] == chip:
                if topo.die(h) == topo.die(core):
                    fwd = q
                else:
                    n[q] = 16
        if fwd is not None:
            sib = [c for c in T.cores if topo.chip(c) == chip and c != core][0]
            srid, spid, _ = topo.addr(sib)
            g.wait_ge(arr[fwd], 8)
            g.remote_dma(T.land[fwd], T.land[fwd], remote_sem=arr[fwd], local_sem=T.sem.snt,
                         pid=spid, routing_id=srid, dma_engine_mask=0xFFFF)
            sent += 16
            qs[fwd].wait_ge(T.sem.snt, sent)
        cnt = [0, 0]
        for q in (0, 1):
            qs[q].wait_ge(arr[q], n[q])
            for s in range(6):
                r = 2 * s + q
                if r == rank:
                    continue
                qs[q].dma_start(T.y[:, r * W:(r + 1) * W], T.land[q, :, s * W:(s + 1) * W]).then_inc(st[q], 16)
                cnt[q] += 16
        g.wait_ge(T.sem.snt, sent)
        g.sync.wait_ge(T.sem.st0, cnt[0])
        g.scalar.wait_ge(T.sem.st1, cnt[1])
        g.scalar.wait_ge(T.sem.own, 16)
        return

    if core in SERVE:
        par = chip & 1
        own, mate, third = SERVE[core]
        srcs = [c for c in T.cores if (topo.chip(c) & 1) == par]
        g.wait_ge(T.sem.inn, sum(_bits(_mask(topo, c, core)) for c in srcs))
        arr = T.sem.arr0 if par == 0 else T.sem.arr1
        out = T.land[par]
        first = [c for c in T.cores if topo.chip(c) == third and topo.die(c) == topo.die(core)][0]
        off = [c for c in T.cores if topo.chip(c) == mate]
        on = [c for c in T.cores if topo.chip(c) == own]
        frid, fpid, _ = topo.addr(first)
        g.remote_dma(out, T.G[:], remote_sem=arr, local_sem=T.sem.snt,
                     pid=fpid, routing_id=frid, dma_engine_mask=0x00FF)
        g.remote_dma_fused([
            RemoteDMATransfer(dst_ids=[_dst(topo, c) for c in off], dma_engine_mask=0x00FF, remote_sem=arr,
                              srcs=[T.G[:]], dsts=[out for _ in off]),
            RemoteDMATransfer(dst_ids=[_dst(topo, c) for c in on], dma_engine_mask=0xFF00, remote_sem=arr,
                              srcs=[T.G[:]], dsts=[out for _ in on]),
        ], local_sem=T.sem.snt)
        g.wait_ge(T.sem.snt, 8 + 8 + 8)
